import numpy as np
import ml_dtypes


def mxq(x, axis, fmt="e4m3"):
    dtype, down = {"e4m3": (ml_dtypes.float8_e4m3fn, 7), "e5m2": (ml_dtypes.float8_e5m2, 14)}[fmt]
    v = np.moveaxis(np.asarray(x, np.float32).astype(ml_dtypes.bfloat16).astype(np.float64), axis, -1)
    blocks = v.reshape(v.shape[:-1] + (-1, 32))
    amax = np.abs(blocks).max(-1, keepdims=True)
    byte = np.maximum(np.where(amax > 0, np.frexp(amax)[1] - 1 + 127, 0) - down, 1)
    scale = np.exp2(byte - 127.0)
    codes = (blocks / scale).astype(np.float32).astype(dtype).astype(np.float64)
    return np.moveaxis((codes * scale).reshape(v.shape), -1, axis)


WIDE = False


def mx_kscale(k):
    if not WIDE:
        return np.ones(k)
    levels = np.array([10, -10, 5, -5, 0])
    if k % 512:
        return np.exp2(np.random.permutation(np.resize(levels, k // 32))).repeat(32)
    a = np.empty((k // 512, 16))
    for p in range(k // 512):
        a[p, :8] = np.random.permutation(np.resize(levels, 8))
        for g in range(8):
            far = levels[np.abs(levels - a[p, g]) >= 10]
            a[p, g + 8] = far[np.random.randint(len(far))]
    return np.exp2(a.ravel()).repeat(32)


BF16 = ml_dtypes.bfloat16


def bf(x):
    return np.asarray(x, np.float32).astype(BF16)


def f64(x):
    return np.asarray(x).astype(np.float64)


M, K, D, T = 2048, 1024, 1024, 512


def draw0():
    s, t = mx_kscale(K), mx_kscale(M)
    return {"x": bf(np.random.standard_normal((M, K)) * s),
            "omega": bf(np.random.standard_normal((K, D)) / np.sqrt(K) / s[:, None]),
            "inv_width": bf(1 + 0.1 * np.random.standard_normal(D)),
            "phase": bf(0.5 * np.random.standard_normal(D)),
            "sample_w": bf((1 + 0.2 * np.random.standard_normal(M)) * t),
            "y": bf(np.random.standard_normal((M, T)) / np.sqrt(M) / t[:, None]),
            "ridge": bf(0.25 + 0.1 * np.abs(np.random.standard_normal(D))),
            "theta_cos": bf(0.5 * np.random.standard_normal((D, T))),
            "theta_sin": bf(0.5 * np.random.standard_normal((D, T)))}


def core(x, omega, inv_width, phase, sample_w, y, ridge, theta_cos, theta_sin):
    z = mxq(f64(x), 1, "e4m3") @ mxq(f64(omega), 0, "e4m3")
    angle = z * f64(inv_width) + f64(phase)
    fc = np.cos(angle)
    fs = np.sin(angle)
    ec = np.mean(fc * fc, axis=0)
    es = np.mean(fs * fs, axis=0)
    r = f64(sample_w)[:, None]
    yq = mxq(f64(y), 0, "e4m3")
    hc = mxq(fc * r, 0, "e4m3")
    hs = mxq(fs * r, 0, "e4m3")
    mc = hc.T @ yq
    ms = hs.T @ yq
    lam = f64(ridge)
    new_cos = f64(theta_cos) + mc / (lam + ec)[:, None]
    new_sin = f64(theta_sin) + ms / (lam + es)[:, None]
    return new_cos, new_sin


def e4m3fn_bytes(y):
    return np.clip(np.asarray(y, np.float64), -448.0, 448.0).astype(np.float32).astype(ml_dtypes.float8_e4m3fn).view(np.uint8)


def e4m3fn_values(b):
    return np.asarray(b, np.uint8).view(ml_dtypes.float8_e4m3fn).astype(np.float64)


def setup_inputs():
    d = draw0()
    x0 = np.asarray(d['x']).astype(np.float64)
    s = (np.max(np.abs(x0), axis=(0,), keepdims=True) / 448.0).astype(np.float32)
    out = {}
    for k, v in d.items():
        if k == 'x':
            out['x_bytes'] = e4m3fn_bytes(x0 / s.astype(np.float64))
            out['x_scale'] = s
        else:
            out[k] = v
    return out


def reference(x_bytes, x_scale, omega, inv_width, phase, sample_w, y, ridge, theta_cos, theta_sin):
    return core(e4m3fn_values(x_bytes) * x_scale.astype(np.float64), omega, inv_width, phase, sample_w, y, ridge, theta_cos, theta_sin)

@@ -1,0 +1,352 @@
+from contextlib import ExitStack
+import math
+
+import concourse.mybir as mybir
+from concourse.masks import make_identity
+
+M, K, D, T = 2048, 1024, 1024, 512
+FLOPS = 2 * M * K * D + 2 * 2 * M * D * T
+
+F32 = mybir.dt.float32
+BF16 = mybir.dt.bfloat16
+I32 = mybir.dt.int32
+U32 = mybir.dt.uint32
+U8 = mybir.dt.uint8
+FP8 = mybir.dt.float8_e4m3fn
+FP8X4 = mybir.dt.float8_e4m3fn_x4
+ACT = mybir.ActivationFunctionType
+ALU = mybir.AluOpType
+
+P = 128
+G = 4
+ND = 8
+TWO_PI = 2.0 * math.pi
+
+
+def tile_fourier_feature_regression_f4_kernel(
+    tc, x_bytes, x_scale, omega, inv_width, phase, sample_w, y, ridge, theta_cos, theta_sin, out_0, out_1
+):
+    nc = tc.nc
+    with ExitStack() as ctx:
+        keep = ctx.enter_context(tc.tile_pool(name="keep", bufs=1))
+        stream = ctx.enter_context(tc.tile_pool(name="stream", bufs=2))
+        psum = ctx.enter_context(tc.psum_pool(name="psum", bufs=2))
+
+        def kt(shape, dtype, name):
+            return keep.tile(shape, dtype, name=name, align_bytes=64)
+
+        ctx.enter_context(tc.manual_schedule())
+
+        scale_bc = kt([P, K], F32, "scale_bc")
+        nc.scalar.dma_start(out=scale_bc[:], in_=x_scale.rearrange("o k -> (o k)").partition_broadcast(P))
+        xraw = [kt([P, 4 * K], U8, f"xraw{g}") for g in range(G)]
+        oraw = {}
+        for h in range(2):
+            for q in range(2):
+                oraw[(q, h)] = kt([P, 4, 512], BF16, f"oraw{q}{h}")
+        yraw = [kt([P, 4, T], BF16, f"yraw{g}") for g in range(G)]
+        th = [kt([P, ND, T], BF16, f"theta{c}") for c in range(2)]
+
+        def load_x(g):
+            nc.sync.dma_start(out=xraw[g][:], in_=x_bytes[512 * g : 512 * (g + 1), :].rearrange("(p t) k -> p (t k)", t=4))
+
+        def load_o(q, h):
+            nc.sync.dma_start(
+                out=oraw[(q, h)][:],
+                in_=omega[512 * q : 512 * (q + 1), 512 * h : 512 * (h + 1)].rearrange("(p j) d -> p j d", j=4),
+            )
+
+        load_x(0)
+        load_o(0, 0)
+        load_o(1, 0)
+        load_x(1)
+        load_o(0, 1)
+        load_o(1, 1)
+        load_x(2)
+        load_x(3)
+        for g in range(G):
+            nc.sync.dma_start(out=yraw[g][:], in_=y[512 * g : 512 * (g + 1), :].rearrange("(p j) n -> p j n", j=4))
+        nc.sync.dma_start(out=th[0][:], in_=theta_cos.rearrange("(d p) n -> p d n", p=P))
+        nc.sync.dma_start(out=th[1][:], in_=theta_sin.rearrange("(d p) n -> p d n", p=P))
+
+        ident_f = kt([P, P], F32, "ident_f")
+        ident_b = kt([P, P], BF16, "ident_b")
+        vec_rows = kt([P, P], BF16, "vec_rows")
+        w_raw = kt([P, 16], BF16, "w_raw")
+        dummy = kt([P, 1], F32, "dummy")
+        nc.gpsimd.memset(vec_rows[:], 0.0)
+        nc.gpsimd.memset(dummy[:], 0.0)
+        nc.scalar.dma_start(out=vec_rows[0:8, :], in_=inv_width.rearrange("(c p) -> c p", p=P))
+        nc.scalar.dma_start(out=vec_rows[8:16, :], in_=phase.rearrange("(c p) -> c p", p=P))
+        nc.scalar.dma_start(out=vec_rows[16:24, :], in_=ridge.rearrange("(c p) -> c p", p=P))
+        nc.scalar.dma_start(
+            out=w_raw[:].rearrange("p (g t) -> p g t", t=4), in_=sample_w.rearrange("(g p t) -> p g t", p=P, t=4)
+        )
+        make_identity(nc, ident_f[:])
+        make_identity(nc, ident_b[:])
+        nc.scalar.activation(dummy[:], dummy[:], ACT.Sin)
+
+        vec = kt([P, 24], F32, "vec")
+        iwt = kt([P, ND], F32, "iwt")
+        pht = kt([P, ND], F32, "pht")
+        phh = kt([P, ND], F32, "phh")
+        rid1 = kt([P, ND], F32, "rid1")
+        w1 = kt([P, 16], F32, "w1")
+        w2 = kt([P, 16], F32, "w2")
+
+        def make_vectors():
+            vt = psum.tile([P, P], BF16, tag="acc", name="vt")
+            nc.tensor.transpose(vt[:], vec_rows[:], ident_b[:])
+            nc.vector.tensor_copy(out=vec[:], in_=vt[:, 0:24])
+            nc.vector.tensor_scalar(iwt[:], vec[:, 0:8], 1.0 / TWO_PI, None, ALU.mult)
+            nc.vector.tensor_scalar(pht[:], vec[:, 8:16], 1.0 / TWO_PI, None, ALU.mult)
+            nc.vector.tensor_scalar(phh[:], vec[:, 8:16], 0.5, None, ALU.mult)
+            nc.vector.tensor_scalar(rid1[:], vec[:, 16:24], 1.0, None, ALU.add)
+            nc.vector.tensor_copy(out=w1[:], in_=w_raw[:])
+            nc.vector.tensor_scalar(w2[:], w_raw[:], -2.0, None, ALU.mult)
+
+        oc = [kt([P, D], U32, f"oc{q}") for q in range(2)]
+        osc = [kt([P, D], U8, f"os{q}") for q in range(2)]
+        oin = {}
+
+        def o_interleave(q, h, eng):
+            t = stream.tile([P, 2048], BF16, tag="qin", name=f"oin{q}{h}", align_bytes=64, bufs=5)
+            oin[(q, h)] = t
+            dst = t[:].rearrange("p (d j) -> p d j", j=4)
+            src = oraw[(q, h)][:].rearrange("p j d -> p d j")
+            if eng == "s":
+                nc.scalar.copy(out=dst, in_=src)
+            else:
+                nc.gpsimd.tensor_scalar(dst, src, 1.0, 0.0, ALU.mult, ALU.add)
+
+        def o_quant(q, h):
+            c = slice(512 * h, 512 * (h + 1))
+            nc.vector.quantize_mx(out=oc[q][:, c].bitcast(FP8X4), scales=osc[q][:, c], in_=oin[(q, h)][:])
+
+        yc = [kt([P, T], U32, f"yc{g}") for g in range(G)]
+        ys = [kt([P, T], U8, f"ys{g}") for g in range(G)]
+        yin = {}
+
+        def y_interleave(g):
+            t = stream.tile([P, 2048], BF16, tag="qin", name=f"yin{g}", align_bytes=64, bufs=5)
+            yin[g] = t
+            nc.gpsimd.tensor_scalar(
+                t[:].rearrange("p (n j) -> p n j", j=4), yraw[g][:].rearrange("p j n -> p n j"), 1.0, 0.0, ALU.mult, ALU.add
+            )
+
+        def y_quant(g):
+            nc.vector.quantize_mx(out=yc[g][:].bitcast(FP8X4), scales=ys[g][:], in_=yin[g][:])
+
+        xb, xin = {}, {}
+        xc = {}
+        xs = {}
+        for g in range(G):
+            for q in range(2):
+                xc[(g, q)] = kt([P, 512], U32, f"xc{g}{q}")
+                xs[(g, q)] = kt([P, 512], U8, f"xs{g}{q}")
+
+        def x_widen(g, t):
+            if t == 0:
+                xb[g] = stream.tile([P, 4 * K], BF16, tag="xb", name=f"xb{g}", align_bytes=64, bufs=2)
+            c = slice(K * t, K * (t + 1))
+            nc.vector.tensor_tensor(xb[g][:, c], xraw[g][:, c].bitcast(FP8), scale_bc[:], ALU.mult)
+
+        def x_transpose(g, q, h):
+            if h == 0:
+                xin[(g, q)] = stream.tile([P, 2048], BF16, tag="qin", name=f"xin{g}{q}", align_bytes=64, bufs=5)
+            words = xb[g][:].bitcast(F32)
+            bank = psum.tile([P, 2, 2, P], F32, tag="acc", name=f"xt{g}{q}{h}")
+            for a in range(2):
+                for u in range(2):
+                    base = 512 * (2 * h + a) + 256 * q
+                    nc.tensor.transpose(bank[:, a, u, :], words[:, base + u : base + 256 : 2], ident_f[:])
+            dst = xin[(g, q)][:].bitcast(F32)[:, 512 * h : 512 * (h + 1)]
+            nc.scalar.copy(out=dst.rearrange("p (a r u) -> p a r u", a=2, u=2), in_=bank[:].rearrange("p a u r -> p a r u"))
+
+        def x_quant(g, q):
+            nc.vector.quantize_mx(out=xc[(g, q)][:].bitcast(FP8X4), scales=xs[(g, q)][:], in_=xin[(g, q)][:])
+
+        units = [(0, d) for d in range(ND)] + [(1, d) for d in range(ND)]
+        for d in range(ND):
+            units += [(2, d), (3, d)]
+        n_units = len(units)
+        via_gpsimd = [i for i in range(n_units) if i not in (0, 1, 20, 28)]
+        zb, nb, vb, sb, hb, qb, fs, fq, hin = {}, {}, {}, {}, {}, {}, {}, {}, {}
+        hcod, hsc = {}, {}
+        for u in units:
+            hcod[u] = kt([P, 256], U32, f"hc{u[0]}{u[1]}")
+            hsc[u] = kt([P, 256], U8, f"hs{u[0]}{u[1]}")
+        stats = [kt([P, G], F32, f"stats{d}") for d in range(ND)]
+
+        def z_mm(i):
+            g, d = units[i]
+            zb[i] = psum.tile([P, 512], F32, tag="z", name=f"z{i}", bufs=3)
+            for q in range(2):
+                c = slice(P * d, P * (d + 1))
+                nc.tensor.matmul_mx(
+                    out=zb[i][:], lhsT=oc[q][:, c].bitcast(FP8X4), lhsT_scale=osc[q][:, c],
+                    rhs=xc[(g, q)][:].bitcast(FP8X4), rhs_scale=xs[(g, q)][:], start=(q == 0), stop=(q == 1),
+                )
+
+        def rr1(i):
+            d = units[i][1]
+            nb[i] = stream.tile([P, 512], I32, tag="n", name=f"n{i}")
+            if i in via_gpsimd:
+                u = stream.tile([P, 512], F32, tag="u", name=f"u{i}", bufs=2)
+                nc.scalar.activation(u[:], zb[i][:], ACT.Identity, bias=pht[:, d : d + 1], scale=iwt[:, d : d + 1])
+                nc.gpsimd.tensor_scalar(nb[i][:], u[:], 1.0, 0.0, ALU.mult, ALU.add)
+            else:
+                nc.vector.tensor_scalar(nb[i][:], zb[i][:], iwt[:, d : d + 1], pht[:, d : d + 1], ALU.mult, ALU.add)
+
+        def rr2(i):
+            d = units[i][1]
+            vb[i] = stream.tile([P, 512], F32, tag="v", name=f"v{i}", bufs=3)
+            nc.vector.scalar_tensor_tensor(vb[i][:], zb[i][:], iwt[:, d : d + 1], nb[i][:], ALU.mult, ALU.subtract)
+
+        def trig(i):
+            g, d = units[i]
+            hb[i] = stream.tile([P, 512], F32, tag="half", name=f"half{i}", bufs=2)
+            sb[i] = stream.tile([P, 512], F32, tag="sin", name=f"sin{i}", bufs=2)
+            qb[i] = stream.tile([P, 512], F32, tag="q", name=f"q{i}", bufs=2)
+            junk = stream.tile([P, 512], BF16, tag="junk", name=f"junk{i}", bufs=2)
+            nc.scalar.activation(sb[i][:], vb[i][:], ACT.Sin, bias=vec[:, 8 + d : 9 + d], scale=TWO_PI)
+            nc.scalar.activation(hb[i][:], vb[i][:], ACT.Sin, bias=phh[:, d : d + 1], scale=math.pi)
+            nc.scalar.activation(junk[:], sb[i][:], ACT.Square, accum_out=stats[d][:, g : g + 1])
+            nc.scalar.activation(qb[i][:], hb[i][:], ACT.Square)
+
+        def f_trans(i):
+            fs[i] = psum.tile([P, 4, P], F32, tag="f", name=f"fs{i}", bufs=3)
+            for t in range(4):
+                nc.tensor.transpose(fs[i][:, t, :], sb[i][:, P * t : P * (t + 1)], ident_f[:])
+            fq[i] = psum.tile([P, 4, P], F32, tag="f", name=f"fq{i}", bufs=3)
+            for t in range(4):
+                nc.tensor.transpose(fq[i][:, t, :], qb[i][:, P * t : P * (t + 1)], ident_f[:])
+
+        def w_s(i):
+            g = units[i][0]
+            hin[i] = stream.tile([P, 1024], BF16, tag="hin", name=f"hin{i}", align_bytes=64, bufs=3)
+            nc.vector.tensor_tensor(
+                hin[i][:, 512:1024].rearrange("p (d t) -> p d t", t=4),
+                fs[i][:].rearrange("p t d -> p d t"),
+                w1[:, 4 * g : 4 * g + 4].unsqueeze(1).to_broadcast([P, P, 4]),
+                ALU.mult,
+            )
+
+        def w_c(i):
+            g = units[i][0]
+            nc.vector.scalar_tensor_tensor(
+                hin[i][:, 0:512].rearrange("p (d t) -> p d t", t=4),
+                fq[i][:].rearrange("p t d -> p d t"),
+                0.5,
+                w2[:, 4 * g : 4 * g + 4].unsqueeze(1).to_broadcast([P, P, 4]),
+                ALU.subtract,
+                ALU.mult,
+            )
+
+        def f_quant(i):
+            u = units[i]
+            nc.vector.quantize_mx(out=hcod[u][:].bitcast(FP8X4), scales=hsc[u][:], in_=hin[i][:])
+
+        acc, rec = {}, {}
+
+        def moments(d):
+            for c in range(2):
+                acc[(c, d)] = psum.tile([P, T], F32, tag="acc", name=f"acc{c}{d}")
+                cols = slice(P * c, P * (c + 1))
+                for g in range(G):
+                    nc.tensor.matmul_mx(
+                        out=acc[(c, d)][:], lhsT=hcod[(g, d)][:, cols].bitcast(FP8X4), lhsT_scale=hsc[(g, d)][:, cols],
+                        rhs=yc[g][:].bitcast(FP8X4), rhs_scale=ys[g][:], start=(g == 0), stop=(g == G - 1),
+                    )
+
+        def denominators(d):
+            es = stream.tile([P, 1], F32, tag="es", name=f"es{d}")
+            den = stream.tile([P, 2], F32, tag="den", name=f"den{d}")
+            rec[d] = stream.tile([P, 2], F32, tag="rec", name=f"rec{d}", bufs=3)
+            es2 = stream.tile([P, 2], F32, tag="es2", name=f"es2{d}")
+            nc.gpsimd.tensor_tensor(es2[:], stats[d][:, 0:2], stats[d][:, 2:4], ALU.add)
+            nc.gpsimd.tensor_tensor(es[:], es2[:, 0:1], es2[:, 1:2], ALU.add)
+            nc.gpsimd.tensor_scalar(den[:, 0:1], es[:], -1.0 / M, rid1[:, d : d + 1], ALU.mult, ALU.add)
+            nc.gpsimd.tensor_scalar(den[:, 1:2], es[:], 1.0 / M, vec[:, 16 + d : 17 + d], ALU.mult, ALU.add)
+            nc.vector.reciprocal(rec[d][:], den[:])
+
+        def epilogue(d):
+            for c in range(2):
+                o = stream.tile([P, T], F32, tag="o", name=f"o{c}{d}", bufs=4)
+                nc.vector.scalar_tensor_tensor(o[:], acc[(c, d)][:], rec[d][:, c : c + 1], th[c][:, d, :], ALU.mult, ALU.add)
+                nc.sync.dma_start(out=(out_0, out_1)[c][P * d : P * (d + 1), :], in_=o[:])
+
+        o_interleave(0, 0, "s")
+        o_interleave(1, 0, "s")
+        x_widen(0, 0)
+        x_widen(0, 1)
+        x_transpose(0, 0, 0)
+        x_transpose(0, 1, 0)
+        x_widen(0, 2)
+        x_widen(0, 3)
+        x_transpose(0, 0, 1)
+        x_transpose(0, 1, 1)
+        x_widen(1, 0)
+        make_vectors()
+        o_quant(0, 0)
+        o_quant(1, 0)
+        x_quant(0, 0)
+        x_quant(0, 1)
+        o_interleave(0, 1, "g")
+        o_interleave(1, 1, "g")
+        for g in range(G):
+            y_interleave(g) if g < 2 else None
+        z_mm(0)
+        z_mm(1)
+        rr1(0)
+
+        extra_v = {}
+        extra_x = {}
+
+        def at(table, step, fn, *args):
+            table.setdefault(step, []).append((fn, args))
+
+        at(extra_v, 1, o_quant, 0, 1)
+        at(extra_v, 1, o_quant, 1, 1)
+        for g, a0 in ((1, -1), (2, 5), (3, 8)):
+            for t in range(4):
+                at(extra_v, a0 + t, x_widen, g, t)
+            at(extra_x, a0 + 2, x_transpose, g, 0, 0)
+            at(extra_x, a0 + 3, x_transpose, g, 1, 0)
+            at(extra_x, a0 + 4, x_transpose, g, 0, 1)
+            at(extra_x, a0 + 5, x_transpose, g, 1, 1)
+            at(extra_v, a0 + 5, x_quant, g, 0)
+            at(extra_v, a0 + 6, x_quant, g, 1)
+        at(extra_v, 7, y_quant, 0)
+        at(extra_v, 8, y_quant, 1)
+        at(extra_x, 9, y_interleave, 2)
+        at(extra_x, 10, y_interleave, 3)
+        at(extra_v, 14, y_quant, 2)
+        at(extra_v, 15, y_quant, 3)
+
+        for i in range(n_units + 5):
+            if i + 2 < n_units:
+                z_mm(i + 2)
+            if i + 1 < n_units:
+                rr1(i + 1)
+            if 0 <= i - 2 < n_units:
+                w_s(i - 2)
+            if i < n_units:
+                rr2(i)
+                trig(i)
+            for fn, args in extra_x.get(i, []):
+                fn(*args)
+            if 0 <= i - 1 < n_units:
+                f_trans(i - 1)
+            if 0 <= i - 2 < n_units:
+                w_c(i - 2)
+            for fn, args in extra_v.get(i, []):
+                fn(*args)
+            if 0 <= i - 3 < n_units:
+                f_quant(i - 3)
+                g, d = units[i - 3]
+                if g == 3:
+                    moments(d)
+                    denominators(d)
+            if 0 <= i - 4 < n_units and units[i - 4][0] == 3:
+                epilogue(units[i - 4][1])

@@ -23,6 +23,9 @@ ND = 8
 TWO_PI = 2.0 * math.pi
 
 
+PRM = {'man': 1, 'via_g': [0, 1, 2, 3, 6, 7, 10, 11, 12, 13, 14, 15, 18, 20, 23, 24, 25, 27, 28, 29, 31], 'oe': 'ssssvsvv', 'o1': 0, 'x': [[(0, 0, 1, 3), (0, 3, 3, 4), (5, 5)], [(4, 4, 5, 8), (4, 8, 8, 10), (10, 11)], [(8, 11, 12, 13), (11, 11, 13, 13), (14, 14)]], 'y': (2, 14, 17, 10), 'ye': 'ssvv', 'qe': {}}
+
+
 def tile_fourier_feature_regression_f4_kernel(
     tc, x_bytes, x_scale, omega, inv_width, phase, sample_w, y, ridge, theta_cos, theta_sin, out_0, out_1
 ):
@@ -35,40 +38,10 @@ def tile_fourier_feature_regression_f4_kernel(
         def kt(shape, dtype, name):
             return keep.tile(shape, dtype, name=name, align_bytes=64)
 
-        ctx.enter_context(tc.manual_schedule())
+        if PRM["man"]:
+            ctx.enter_context(tc.manual_schedule())
 
         scale_bc = kt([P, K], F32, "scale_bc")
-        nc.scalar.dma_start(out=scale_bc[:], in_=x_scale.rearrange("o k -> (o k)").partition_broadcast(P))
-        xraw = [kt([P, 4 * K], U8, f"xraw{g}") for g in range(G)]
-        oraw = {}
-        for h in range(2):
-            for q in range(2):
-                oraw[(q, h)] = kt([P, 4, 512], BF16, f"oraw{q}{h}")
-        yraw = [kt([P, 4, T], BF16, f"yraw{g}") for g in range(G)]
-        th = [kt([P, ND, T], BF16, f"theta{c}") for c in range(2)]
-
-        def load_x(g):
-            nc.sync.dma_start(out=xraw[g][:], in_=x_bytes[512 * g : 512 * (g + 1), :].rearrange("(p t) k -> p (t k)", t=4))
-
-        def load_o(q, h):
-            nc.sync.dma_start(
-                out=oraw[(q, h)][:],
-                in_=omega[512 * q : 512 * (q + 1), 512 * h : 512 * (h + 1)].rearrange("(p j) d -> p j d", j=4),
-            )
-
-        load_x(0)
-        load_o(0, 0)
-        load_o(1, 0)
-        load_x(1)
-        load_o(0, 1)
-        load_o(1, 1)
-        load_x(2)
-        load_x(3)
-        for g in range(G):
-            nc.sync.dma_start(out=yraw[g][:], in_=y[512 * g : 512 * (g + 1), :].rearrange("(p j) n -> p j n", j=4))
-        nc.sync.dma_start(out=th[0][:], in_=theta_cos.rearrange("(d p) n -> p d n", p=P))
-        nc.sync.dma_start(out=th[1][:], in_=theta_sin.rearrange("(d p) n -> p d n", p=P))
-
         ident_f = kt([P, P], F32, "ident_f")
         ident_b = kt([P, P], BF16, "ident_b")
         vec_rows = kt([P, P], BF16, "vec_rows")
@@ -76,15 +49,55 @@ def tile_fourier_feature_regression_f4_kernel(
         dummy = kt([P, 1], F32, "dummy")
         nc.gpsimd.memset(vec_rows[:], 0.0)
         nc.gpsimd.memset(dummy[:], 0.0)
-        nc.scalar.dma_start(out=vec_rows[0:8, :], in_=inv_width.rearrange("(c p) -> c p", p=P))
-        nc.scalar.dma_start(out=vec_rows[8:16, :], in_=phase.rearrange("(c p) -> c p", p=P))
-        nc.scalar.dma_start(out=vec_rows[16:24, :], in_=ridge.rearrange("(c p) -> c p", p=P))
+        make_identity(nc, ident_b[:])
+        make_identity(nc, ident_f[:])
+        for j, vector in enumerate((inv_width, phase, ridge)):
+            nc.scalar.dma_start(out=vec_rows[8 * j : 8 * j + 8, :], in_=vector.rearrange("(c p) -> c p", p=P))
         nc.scalar.dma_start(
             out=w_raw[:].rearrange("p (g t) -> p g t", t=4), in_=sample_w.rearrange("(g p t) -> p g t", p=P, t=4)
         )
-        make_identity(nc, ident_f[:])
-        make_identity(nc, ident_b[:])
+        nc.scalar.dma_start(out=scale_bc[:], in_=x_scale.rearrange("o k -> (o k)").partition_broadcast(P))
         nc.scalar.activation(dummy[:], dummy[:], ACT.Sin)
+
+        xraw = [kt([P, 4 * K], U8, f"xraw{g}") for g in range(G)]
+        oraw = {}
+        for q in range(2):
+            for h in range(2):
+                oraw[(q, h)] = stream.tile([P, 4, 512], BF16, tag="raw", name=f"oraw{q}{h}", bufs=6)
+        yraw = {}
+        th = [kt([P, ND, T], BF16, f"theta{c}") for c in range(2)]
+
+        def load_x(g, t0=0, t1=4):
+            nc.sync.dma_start(
+                out=xraw[g][:, K * t0 : K * t1],
+                in_=x_bytes[512 * g : 512 * (g + 1), :].rearrange("(p t) k -> p (t k)", t=4)[:, K * t0 : K * t1],
+            )
+
+        def load_o(q, h):
+            nc.sync.dma_start(
+                out=oraw[(q, h)][:],
+                in_=omega[512 * q : 512 * (q + 1), 512 * h : 512 * (h + 1)].rearrange("(p j) d -> p j d", j=4),
+            )
+
+        load_x(0, 0, 2)
+        load_x(0, 2, 4)
+        load_o(0, 0)
+        load_o(1, 0)
+        load_x(1)
+        load_o(0, 1)
+        load_o(1, 1)
+        load_x(2)
+        load_x(3)
+
+        def load_y(g):
+            yraw[g] = stream.tile([P, 4, T], BF16, tag="raw", name=f"yraw{g}", bufs=6)
+            nc.sync.dma_start(out=yraw[g][:], in_=y[512 * g : 512 * (g + 1), :].rearrange("(p j) n -> p j n", j=4))
+
+        def load_theta(c):
+            nc.sync.dma_start(out=th[c][:], in_=(theta_cos, theta_sin)[c].rearrange("(d p) n -> p d n", p=P))
+
+        load_y(0)
+        load_y(1)
 
         vec = kt([P, 24], F32, "vec")
         iwt = kt([P, ND], F32, "iwt")
@@ -98,46 +111,56 @@ def tile_fourier_feature_regression_f4_kernel(
             vt = psum.tile([P, P], BF16, tag="acc", name="vt")
             nc.tensor.transpose(vt[:], vec_rows[:], ident_b[:])
             nc.vector.tensor_copy(out=vec[:], in_=vt[:, 0:24])
+            nc.vector.tensor_copy(out=w1[:], in_=w_raw[:])
+            nc.vector.tensor_scalar(w2[:], w_raw[:], -2.0, None, ALU.mult)
             nc.vector.tensor_scalar(iwt[:], vec[:, 0:8], 1.0 / TWO_PI, None, ALU.mult)
             nc.vector.tensor_scalar(pht[:], vec[:, 8:16], 1.0 / TWO_PI, None, ALU.mult)
             nc.vector.tensor_scalar(phh[:], vec[:, 8:16], 0.5, None, ALU.mult)
             nc.vector.tensor_scalar(rid1[:], vec[:, 16:24], 1.0, None, ALU.add)
-            nc.vector.tensor_copy(out=w1[:], in_=w_raw[:])
-            nc.vector.tensor_scalar(w2[:], w_raw[:], -2.0, None, ALU.mult)
 
-        oc = [kt([P, D], U32, f"oc{q}") for q in range(2)]
-        osc = [kt([P, D], U8, f"os{q}") for q in range(2)]
-        oin = {}
-
-        def o_interleave(q, h, eng):
-            t = stream.tile([P, 2048], BF16, tag="qin", name=f"oin{q}{h}", align_bytes=64, bufs=5)
-            oin[(q, h)] = t
-            dst = t[:].rearrange("p (d j) -> p d j", j=4)
-            src = oraw[(q, h)][:].rearrange("p j d -> p d j")
+        def interleave(dst, raw, eng):
+            dst = dst.rearrange("p (c i j) -> p c j i", i=4, j=4)
+            src = raw.rearrange("p j (c i) -> p c j i", i=4)
             if eng == "s":
                 nc.scalar.copy(out=dst, in_=src)
+            elif eng == "v":
+                nc.vector.tensor_copy(out=dst, in_=src)
             else:
                 nc.gpsimd.tensor_scalar(dst, src, 1.0, 0.0, ALU.mult, ALU.add)
 
-        def o_quant(q, h):
-            c = slice(512 * h, 512 * (h + 1))
-            nc.vector.quantize_mx(out=oc[q][:, c].bitcast(FP8X4), scales=osc[q][:, c], in_=oin[(q, h)][:])
+        qin = {}
+
+        def qin_tile(key):
+            qin[key] = stream.tile([P, 2048], BF16, tag="qin", name="qin_" + "_".join(str(e) for e in key), align_bytes=64, bufs=5)
+            return qin[key]
+
+        oc = [kt([P, D], U32, f"oc{q}") for q in range(2)]
+        osc = [kt([P, D], U8, f"os{q}") for q in range(2)]
+
+        def o_interleave(q, c0, c1, eng):
+            if c1 - c0 < 512:
+                t = stream.tile([P, 1024], BF16, tag="qsmall", name=f"qsmall{q}{c0}", align_bytes=64, bufs=4)
+                qin[("o", q, c0)] = t
+            else:
+                t = qin_tile(("o", q, c0))
+            interleave(t[:, 0 : 4 * (c1 - c0)], oraw[(q, c0 // 512)][:, :, c0 % 512 : c0 % 512 + c1 - c0], eng)
+
+        def o_quant(q, c0, c1):
+            nc.vector.quantize_mx(
+                out=oc[q][:, c0:c1].bitcast(FP8X4), scales=osc[q][:, c0:c1], in_=qin[("o", q, c0)][:, 0 : 4 * (c1 - c0)]
+            )
 
         yc = [kt([P, T], U32, f"yc{g}") for g in range(G)]
         ys = [kt([P, T], U8, f"ys{g}") for g in range(G)]
-        yin = {}
 
-        def y_interleave(g):
-            t = stream.tile([P, 2048], BF16, tag="qin", name=f"yin{g}", align_bytes=64, bufs=5)
-            yin[g] = t
-            nc.gpsimd.tensor_scalar(
-                t[:].rearrange("p (n j) -> p n j", j=4), yraw[g][:].rearrange("p j n -> p n j"), 1.0, 0.0, ALU.mult, ALU.add
-            )
+        def y_interleave(g, eng):
+            t = qin_tile(("y", g))
+            interleave(t[:], yraw[g][:], eng)
 
         def y_quant(g):
-            nc.vector.quantize_mx(out=yc[g][:].bitcast(FP8X4), scales=ys[g][:], in_=yin[g][:])
+            nc.vector.quantize_mx(out=yc[g][:].bitcast(FP8X4), scales=ys[g][:], in_=qin[("y", g)][:])
 
-        xb, xin = {}, {}
+        xb = {}
         xc = {}
         xs = {}
         for g in range(G):
@@ -151,82 +174,114 @@ def tile_fourier_feature_regression_f4_kernel(
             c = slice(K * t, K * (t + 1))
             nc.vector.tensor_tensor(xb[g][:, c], xraw[g][:, c].bitcast(FP8), scale_bc[:], ALU.mult)
 
-        def x_transpose(g, q, h):
+        def x_transpose(g, q, h, eng="s"):
             if h == 0:
-                xin[(g, q)] = stream.tile([P, 2048], BF16, tag="qin", name=f"xin{g}{q}", align_bytes=64, bufs=5)
+                qin_tile(("x", g, q))
             words = xb[g][:].bitcast(F32)
             bank = psum.tile([P, 2, 2, P], F32, tag="acc", name=f"xt{g}{q}{h}")
             for a in range(2):
                 for u in range(2):
                     base = 512 * (2 * h + a) + 256 * q
                     nc.tensor.transpose(bank[:, a, u, :], words[:, base + u : base + 256 : 2], ident_f[:])
-            dst = xin[(g, q)][:].bitcast(F32)[:, 512 * h : 512 * (h + 1)]
-            nc.scalar.copy(out=dst.rearrange("p (a r u) -> p a r u", a=2, u=2), in_=bank[:].rearrange("p a u r -> p a r u"))
+            dst = qin[("x", g, q)][:].bitcast(F32)[:, 512 * h : 512 * (h + 1)].rearrange("p (a r u) -> p a r u", a=2, u=2)
+            if eng == "s":
+                nc.scalar.copy(out=dst, in_=bank[:].rearrange("p a u r -> p a r u"))
+            else:
+                nc.vector.tensor_copy(out=dst, in_=bank[:].rearrange("p a u r -> p a r u"))
 
-        def x_quant(g, q):
-            nc.vector.quantize_mx(out=xc[(g, q)][:].bitcast(FP8X4), scales=xs[(g, q)][:], in_=xin[(g, q)][:])
+        def x_quant(g, q, lo=0, hi=512):
+            nc.vector.quantize_mx(
+                out=xc[(g, q)][:, lo:hi].bitcast(FP8X4), scales=xs[(g, q)][:, lo:hi], in_=qin[("x", g, q)][:, 4 * lo : 4 * hi]
+            )
 
         units = [(0, d) for d in range(ND)] + [(1, d) for d in range(ND)]
         for d in range(ND):
             units += [(2, d), (3, d)]
         n_units = len(units)
-        via_gpsimd = [i for i in range(n_units) if i not in (0, 1, 20, 28)]
+        last = n_units - 1
         zb, nb, vb, sb, hb, qb, fs, fq, hin = {}, {}, {}, {}, {}, {}, {}, {}, {}
         hcod, hsc = {}, {}
         for u in units:
             hcod[u] = kt([P, 256], U32, f"hc{u[0]}{u[1]}")
             hsc[u] = kt([P, 256], U8, f"hs{u[0]}{u[1]}")
-        stats = [kt([P, G], F32, f"stats{d}") for d in range(ND)]
+        stats = [kt([P, 2 * G], F32, f"stats{d}") for d in range(ND)]
 
-        def z_mm(i):
+        def z_mm(i, lo=0, hi=512):
             g, d = units[i]
-            zb[i] = psum.tile([P, 512], F32, tag="z", name=f"z{i}", bufs=3)
+            if lo == 0:
+                zb[i] = psum.tile([P, 512], F32, tag="z", name=f"z{i}", bufs=3)
+            c = slice(P * d, P * (d + 1))
             for q in range(2):
-                c = slice(P * d, P * (d + 1))
                 nc.tensor.matmul_mx(
-                    out=zb[i][:], lhsT=oc[q][:, c].bitcast(FP8X4), lhsT_scale=osc[q][:, c],
-                    rhs=xc[(g, q)][:].bitcast(FP8X4), rhs_scale=xs[(g, q)][:], start=(q == 0), stop=(q == 1),
+                    out=zb[i][:, lo:hi], lhsT=oc[q][:, c].bitcast(FP8X4), lhsT_scale=osc[q][:, c],
+                    rhs=xc[(g, q)][:, lo:hi].bitcast(FP8X4), rhs_scale=xs[(g, q)][:, lo:hi], start=(q == 0), stop=(q == 1),
                 )
 
-        def rr1(i):
+        def rr1(i, lo=0, hi=512):
             d = units[i][1]
-            nb[i] = stream.tile([P, 512], I32, tag="n", name=f"n{i}")
-            if i in via_gpsimd:
+            if lo == 0:
+                nb[i] = stream.tile([P, 512], I32, tag="n", name=f"n{i}")
+            if i in via_g or i in via_v:
                 u = stream.tile([P, 512], F32, tag="u", name=f"u{i}", bufs=2)
-                nc.scalar.activation(u[:], zb[i][:], ACT.Identity, bias=pht[:, d : d + 1], scale=iwt[:, d : d + 1])
-                nc.gpsimd.tensor_scalar(nb[i][:], u[:], 1.0, 0.0, ALU.mult, ALU.add)
+                nc.scalar.activation(u[:, lo:hi], zb[i][:, lo:hi], ACT.Identity, bias=pht[:, d : d + 1], scale=iwt[:, d : d + 1])
+                if i in via_g:
+                    nc.gpsimd.tensor_scalar(nb[i][:, lo:hi], u[:, lo:hi], 1.0, 0.0, ALU.mult, ALU.add)
+                else:
+                    nc.vector.tensor_copy(out=nb[i][:, lo:hi], in_=u[:, lo:hi])
             else:
-                nc.vector.tensor_scalar(nb[i][:], zb[i][:], iwt[:, d : d + 1], pht[:, d : d + 1], ALU.mult, ALU.add)
+                nc.vector.tensor_scalar(
+                    nb[i][:, lo:hi], zb[i][:, lo:hi], iwt[:, d : d + 1], pht[:, d : d + 1], ALU.mult, ALU.add
+                )
 
-        def rr2(i):
+        def rr2(i, lo=0, hi=512):
             d = units[i][1]
-            vb[i] = stream.tile([P, 512], F32, tag="v", name=f"v{i}", bufs=3)
-            nc.vector.scalar_tensor_tensor(vb[i][:], zb[i][:], iwt[:, d : d + 1], nb[i][:], ALU.mult, ALU.subtract)
+            if lo == 0:
+                vb[i] = stream.tile([P, 512], F32, tag="v", name=f"v{i}", bufs=3)
+            nc.vector.scalar_tensor_tensor(
+                vb[i][:, lo:hi], zb[i][:, lo:hi], iwt[:, d : d + 1], nb[i][:, lo:hi], ALU.mult, ALU.subtract
+            )
 
-        def trig(i):
-            g, d = units[i]
-            hb[i] = stream.tile([P, 512], F32, tag="half", name=f"half{i}", bufs=2)
-            sb[i] = stream.tile([P, 512], F32, tag="sin", name=f"sin{i}", bufs=2)
+        def sines(i, lo=0, hi=512):
+            d = units[i][1]
+            if lo == 0:
+                hb[i] = stream.tile([P, 512], F32, tag="half", name=f"half{i}", bufs=2)
+                sb[i] = stream.tile([P, 512], F32, tag="sin", name=f"sin{i}", bufs=2)
+            nc.scalar.activation(hb[i][:, lo:hi], vb[i][:, lo:hi], ACT.Sin, bias=phh[:, d : d + 1], scale=math.pi)
+            nc.scalar.activation(sb[i][:, lo:hi], vb[i][:, lo:hi], ACT.Sin, bias=vec[:, 8 + d : 9 + d], scale=TWO_PI)
+
+        def square_half(i, eng="s"):
             qb[i] = stream.tile([P, 512], F32, tag="q", name=f"q{i}", bufs=2)
-            junk = stream.tile([P, 512], BF16, tag="junk", name=f"junk{i}", bufs=2)
-            nc.scalar.activation(sb[i][:], vb[i][:], ACT.Sin, bias=vec[:, 8 + d : 9 + d], scale=TWO_PI)
-            nc.scalar.activation(hb[i][:], vb[i][:], ACT.Sin, bias=phh[:, d : d + 1], scale=math.pi)
-            nc.scalar.activation(junk[:], sb[i][:], ACT.Square, accum_out=stats[d][:, g : g + 1])
-            nc.scalar.activation(qb[i][:], hb[i][:], ACT.Square)
+            if eng == "v":
+                nc.vector.tensor_tensor(qb[i][:], hb[i][:], hb[i][:], ALU.mult)
+            elif eng == "g":
+                nc.gpsimd.tensor_tensor(qb[i][:], hb[i][:], hb[i][:], ALU.mult)
+            else:
+                nc.scalar.activation(qb[i][:], hb[i][:], ACT.Square)
 
-        def f_trans(i):
+        def square_sum(i):
+            g, d = units[i]
+            junk = stream.tile([P, 512], BF16, tag="junk", name=f"junk{i}", bufs=2)
+            nc.scalar.activation(junk[:], sb[i][:], ACT.Square, accum_out=stats[d][:, g : g + 1])
+
+        def trans_s(i):
             fs[i] = psum.tile([P, 4, P], F32, tag="f", name=f"fs{i}", bufs=3)
             for t in range(4):
                 nc.tensor.transpose(fs[i][:, t, :], sb[i][:, P * t : P * (t + 1)], ident_f[:])
+
+        def trans_q(i):
             fq[i] = psum.tile([P, 4, P], F32, tag="f", name=f"fq{i}", bufs=3)
             for t in range(4):
                 nc.tensor.transpose(fq[i][:, t, :], qb[i][:, P * t : P * (t + 1)], ident_f[:])
 
+        def hin_tile(i):
+            if i not in hin:
+                hin[i] = stream.tile([P, 1024], BF16, tag="hin", name=f"hin{i}", align_bytes=64, bufs=3)
+            return hin[i]
+
         def w_s(i):
             g = units[i][0]
-            hin[i] = stream.tile([P, 1024], BF16, tag="hin", name=f"hin{i}", align_bytes=64, bufs=3)
             nc.vector.tensor_tensor(
-                hin[i][:, 512:1024].rearrange("p (d t) -> p d t", t=4),
+                hin_tile(i)[:, 512:1024].rearrange("p (d t) -> p d t", t=4),
                 fs[i][:].rearrange("p t d -> p d t"),
                 w1[:, 4 * g : 4 * g + 4].unsqueeze(1).to_broadcast([P, P, 4]),
                 ALU.mult,
@@ -235,7 +290,7 @@ def tile_fourier_feature_regression_f4_kernel(
         def w_c(i):
             g = units[i][0]
             nc.vector.scalar_tensor_tensor(
-                hin[i][:, 0:512].rearrange("p (d t) -> p d t", t=4),
+                hin_tile(i)[:, 0:512].rearrange("p (d t) -> p d t", t=4),
                 fq[i][:].rearrange("p t d -> p d t"),
                 0.5,
                 w2[:, 4 * g : 4 * g + 4].unsqueeze(1).to_broadcast([P, P, 4]),
@@ -243,110 +298,162 @@ def tile_fourier_feature_regression_f4_kernel(
                 ALU.mult,
             )
 
-        def f_quant(i):
+        def f_quant(i, lo=0, hi=256):
             u = units[i]
-            nc.vector.quantize_mx(out=hcod[u][:].bitcast(FP8X4), scales=hsc[u][:], in_=hin[i][:])
+            nc.vector.quantize_mx(
+                out=hcod[u][:, lo:hi].bitcast(FP8X4), scales=hsc[u][:, lo:hi], in_=hin[i][:, 4 * lo : 4 * hi]
+            )
 
-        acc, rec = {}, {}
+        acc, rec, dens = {}, {}, {}
 
-        def moments(d):
-            for c in range(2):
-                acc[(c, d)] = psum.tile([P, T], F32, tag="acc", name=f"acc{c}{d}")
+        def moments(d, groups=range(G), which=(0, 1)):
+            for c in which:
+                if groups[0] == 0:
+                    acc[(c, d)] = psum.tile([P, T], F32, tag="acc", name=f"acc{c}{d}")
                 cols = slice(P * c, P * (c + 1))
-                for g in range(G):
+                for g in groups:
                     nc.tensor.matmul_mx(
                         out=acc[(c, d)][:], lhsT=hcod[(g, d)][:, cols].bitcast(FP8X4), lhsT_scale=hsc[(g, d)][:, cols],
                         rhs=yc[g][:].bitcast(FP8X4), rhs_scale=ys[g][:], start=(g == 0), stop=(g == G - 1),
                     )
 
         def denominators(d):
-            es = stream.tile([P, 1], F32, tag="es", name=f"es{d}")
-            den = stream.tile([P, 2], F32, tag="den", name=f"den{d}")
+            es = stream.tile([P, 4], F32, tag="es", name=f"es{d}")
+            dens[d] = stream.tile([P, 2], F32, tag="den", name=f"den{d}")
+            nc.gpsimd.tensor_tensor(es[:, 0:2], stats[d][:, 0:2], stats[d][:, 2:4], ALU.add)
+            nc.gpsimd.tensor_tensor(es[:, 2:3], es[:, 0:1], es[:, 1:2], ALU.add)
+            nc.gpsimd.tensor_scalar(dens[d][:, 0:1], es[:, 2:3], -1.0 / M, rid1[:, d : d + 1], ALU.mult, ALU.add)
+            nc.gpsimd.tensor_scalar(dens[d][:, 1:2], es[:, 2:3], 1.0 / M, vec[:, 16 + d : 17 + d], ALU.mult, ALU.add)
+
+        def recip(d):
             rec[d] = stream.tile([P, 2], F32, tag="rec", name=f"rec{d}", bufs=3)
-            es2 = stream.tile([P, 2], F32, tag="es2", name=f"es2{d}")
-            nc.gpsimd.tensor_tensor(es2[:], stats[d][:, 0:2], stats[d][:, 2:4], ALU.add)
-            nc.gpsimd.tensor_tensor(es[:], es2[:, 0:1], es2[:, 1:2], ALU.add)
-            nc.gpsimd.tensor_scalar(den[:, 0:1], es[:], -1.0 / M, rid1[:, d : d + 1], ALU.mult, ALU.add)
-            nc.gpsimd.tensor_scalar(den[:, 1:2], es[:], 1.0 / M, vec[:, 16 + d : 17 + d], ALU.mult, ALU.add)
-            nc.vector.reciprocal(rec[d][:], den[:])
+            nc.vector.reciprocal(rec[d][:], dens[d][:])
 
-        def epilogue(d):
-            for c in range(2):
+        def epilogue(d, which=(0, 1), parts=1):
+            for c in which:
                 o = stream.tile([P, T], F32, tag="o", name=f"o{c}{d}", bufs=4)
-                nc.vector.scalar_tensor_tensor(o[:], acc[(c, d)][:], rec[d][:, c : c + 1], th[c][:, d, :], ALU.mult, ALU.add)
-                nc.sync.dma_start(out=(out_0, out_1)[c][P * d : P * (d + 1), :], in_=o[:])
+                w = T // parts
+                for k in range(parts):
+                    cs = slice(w * k, w * (k + 1))
+                    nc.vector.scalar_tensor_tensor(
+                        o[:, cs], acc[(c, d)][:, cs], rec[d][:, c : c + 1], th[c][:, d, cs], ALU.mult, ALU.add
+                    )
+                    nc.sync.dma_start(out=(out_0, out_1)[c][P * d : P * (d + 1), cs], in_=o[:, cs])
 
-        o_interleave(0, 0, "s")
-        o_interleave(1, 0, "s")
+        via_g = PRM.get("via_g", ())
+        via_v = PRM.get("via_v", ())
+        extra = {}
+
+        def at(step, fn, *args):
+            extra.setdefault(step, []).append((fn, args))
+
+        make_vectors()
         x_widen(0, 0)
         x_widen(0, 1)
+        o_interleave(0, 0, 128, PRM["oe"][0])
+        o_interleave(1, 0, 128, PRM["oe"][1])
         x_transpose(0, 0, 0)
         x_transpose(0, 1, 0)
         x_widen(0, 2)
         x_widen(0, 3)
+        x_quant(0, 0, 0, 256)
+        x_quant(0, 1, 0, 256)
+        o_quant(0, 0, 128)
+        o_quant(1, 0, 128)
         x_transpose(0, 0, 1)
         x_transpose(0, 1, 1)
+        z_mm(0, 0, 256)
         x_widen(1, 0)
-        make_vectors()
-        o_quant(0, 0)
-        o_quant(1, 0)
-        x_quant(0, 0)
-        x_quant(0, 1)
-        o_interleave(0, 1, "g")
-        o_interleave(1, 1, "g")
-        for g in range(G):
-            y_interleave(g) if g < 2 else None
-        z_mm(0)
+        rr1(0, 0, 256)
+        x_quant(0, 0, 256, 512)
+        rr2(0, 0, 256)
+        x_quant(0, 1, 256, 512)
+        z_mm(0, 256, 512)
+        o_interleave(0, 128, 256, PRM["oe"][2])
+        o_interleave(1, 128, 256, PRM["oe"][3])
+        sines(0, 0, 256)
+        x_widen(1, 1)
+        rr1(0, 256, 512)
+        o_quant(0, 128, 256)
+        o_quant(1, 128, 256)
         z_mm(1)
-        rr1(0)
+        rr2(0, 256, 512)
+        sines(0, 256, 512)
+        o_interleave(0, 256, 512, PRM["oe"][4])
+        o_interleave(1, 256, 512, PRM["oe"][5])
+        rr1(1)
+        x_widen(1, 2)
+        o_quant(0, 256, 512)
+        o_quant(1, 256, 512)
+        a = PRM["o1"]
+        at(a, o_interleave, 0, 512, 1024, PRM["oe"][6])
+        at(a, o_interleave, 1, 512, 1024, PRM["oe"][7])
+        at(a + 1, o_quant, 0, 512, 1024)
+        at(a + 1, o_quant, 1, 512, 1024)
+        for g in (2, 3):
+            at(2, load_y, g)
+        for c in range(2):
+            at(2, load_theta, c)
+        for g in (1, 2, 3):
+            ws, ts, qs = PRM["x"][g - 1]
+            for t in range(3 if g == 1 else 0, 4):
+                at(ws[t], x_widen, g, t)
+            for k, (q, h) in enumerate(((0, 0), (1, 0), (0, 1), (1, 1))):
+                at(ts[k], x_transpose, g, q, h)
+            at(qs[0], x_quant, g, 0)
+            at(qs[1], x_quant, g, 1)
+        for g in range(G):
+            at(PRM["y"][g], y_interleave, g, PRM["ye"][g])
+            at(PRM["y"][g] + PRM.get("yl", 2), y_quant, g)
 
-        extra_v = {}
-        extra_x = {}
-
-        def at(table, step, fn, *args):
-            table.setdefault(step, []).append((fn, args))
-
-        at(extra_v, 1, o_quant, 0, 1)
-        at(extra_v, 1, o_quant, 1, 1)
-        for g, a0 in ((1, -1), (2, 5), (3, 8)):
-            for t in range(4):
-                at(extra_v, a0 + t, x_widen, g, t)
-            at(extra_x, a0 + 2, x_transpose, g, 0, 0)
-            at(extra_x, a0 + 3, x_transpose, g, 1, 0)
-            at(extra_x, a0 + 4, x_transpose, g, 0, 1)
-            at(extra_x, a0 + 5, x_transpose, g, 1, 1)
-            at(extra_v, a0 + 5, x_quant, g, 0)
-            at(extra_v, a0 + 6, x_quant, g, 1)
-        at(extra_v, 7, y_quant, 0)
-        at(extra_v, 8, y_quant, 1)
-        at(extra_x, 9, y_interleave, 2)
-        at(extra_x, 10, y_interleave, 3)
-        at(extra_v, 14, y_quant, 2)
-        at(extra_v, 15, y_quant, 3)
-
-        for i in range(n_units + 5):
+        for i in range(n_units + 3):
             if i + 2 < n_units:
                 z_mm(i + 2)
-            if i + 1 < n_units:
+            if 0 < i and i + 1 < n_units:
                 rr1(i + 1)
-            if 0 <= i - 2 < n_units:
+            if 0 <= i - 4 and units[i - 4][0] == 3:
+                moments(units[i - 4][1], [3])
+            if 0 <= i - 2:
                 w_s(i - 2)
             if i < n_units:
-                rr2(i)
-                trig(i)
-            for fn, args in extra_x.get(i, []):
-                fn(*args)
+                if i > 0:
+                    rr2(i)
+                    sines(i)
+                square_half(i, PRM["qe"].get(i, "s") if i < last else "v")
+                square_sum(i)
+                if units[i][0] == 3:
+                    denominators(units[i][1])
             if 0 <= i - 1 < n_units:
-                f_trans(i - 1)
-            if 0 <= i - 2 < n_units:
+                if i - 1 == last:
+                    trans_q(i - 1)
+                    trans_s(i - 1)
+                else:
+                    trans_s(i - 1)
+                    trans_q(i - 1)
+            if 0 <= i - 3 and units[i - 3][0] == 3:
+                moments(units[i - 3][1], [0, 1, 2])
+            if 0 <= i - 2 < last:
                 w_c(i - 2)
-            for fn, args in extra_v.get(i, []):
+            for fn, args in extra.get(i, []):
                 fn(*args)
-            if 0 <= i - 3 < n_units:
+            if 0 <= i - 3:
                 f_quant(i - 3)
-                g, d = units[i - 3]
-                if g == 3:
-                    moments(d)
-                    denominators(d)
-            if 0 <= i - 4 < n_units and units[i - 4][0] == 3:
+                if units[i - 3][0] == 3:
+                    recip(units[i - 3][1])
+            if 0 <= i - 4 and units[i - 4][0] == 3:
                 epilogue(units[i - 4][1])
+            if i == n_units:
+                moments(ND - 2, [3])
+                w_c(last)
+                f_quant(last - 1)
+                epilogue(ND - 2)
+                f_quant(last, 0, 128)
+                moments(ND - 1, [0, 1, 2])
+                w_s(last)
+                recip(ND - 1)
+                moments(ND - 1, [3], [0])
+                f_quant(last, 128, 256)
+                moments(ND - 1, [3], [1])
+                epilogue(ND - 1, [0], 2)
+                epilogue(ND - 1, [1], 2)
+                break

from contextlib import ExitStack
import math

import concourse.mybir as mybir
from concourse.masks import make_identity

M, K, D, T = 2048, 1024, 1024, 512
FLOPS = 2 * M * K * D + 2 * 2 * M * D * T

F32 = mybir.dt.float32
BF16 = mybir.dt.bfloat16
I32 = mybir.dt.int32
U32 = mybir.dt.uint32
U8 = mybir.dt.uint8
FP8 = mybir.dt.float8_e4m3fn
FP8X4 = mybir.dt.float8_e4m3fn_x4
ACT = mybir.ActivationFunctionType
ALU = mybir.AluOpType

P = 128
G = 4
ND = 8
TWO_PI = 2.0 * math.pi


PRM = {'man': 1, 'via_g': [0, 1, 2, 3, 6, 7, 10, 11, 12, 13, 14, 15, 18, 20, 23, 24, 25, 27, 28, 29, 31], 'oe': 'ssssvsvv', 'o1': 0, 'x': [[(0, 0, 1, 3), (0, 3, 3, 4), (5, 5)], [(4, 4, 5, 8), (4, 8, 8, 10), (10, 11)], [(8, 11, 12, 13), (11, 11, 13, 13), (14, 14)]], 'y': (2, 14, 17, 10), 'ye': 'ssvv', 'qe': {}}


def tile_fourier_feature_regression_f4_kernel(
    tc, x_bytes, x_scale, omega, inv_width, phase, sample_w, y, ridge, theta_cos, theta_sin, out_0, out_1
):
    nc = tc.nc
    with ExitStack() as ctx:
        keep = ctx.enter_context(tc.tile_pool(name="keep", bufs=1))
        stream = ctx.enter_context(tc.tile_pool(name="stream", bufs=2))
        psum = ctx.enter_context(tc.psum_pool(name="psum", bufs=2))

        def kt(shape, dtype, name):
            return keep.tile(shape, dtype, name=name, align_bytes=64)

        if PRM["man"]:
            ctx.enter_context(tc.manual_schedule())

        scale_bc = kt([P, K], F32, "scale_bc")
        ident_f = kt([P, P], F32, "ident_f")
        ident_b = kt([P, P], BF16, "ident_b")
        vec_rows = kt([P, P], BF16, "vec_rows")
        w_raw = kt([P, 16], BF16, "w_raw")
        dummy = kt([P, 1], F32, "dummy")
        nc.gpsimd.memset(vec_rows[:], 0.0)
        nc.gpsimd.memset(dummy[:], 0.0)
        make_identity(nc, ident_b[:])
        make_identity(nc, ident_f[:])
        for j, vector in enumerate((inv_width, phase, ridge)):
            nc.scalar.dma_start(out=vec_rows[8 * j : 8 * j + 8, :], in_=vector.rearrange("(c p) -> c p", p=P))
        nc.scalar.dma_start(
            out=w_raw[:].rearrange("p (g t) -> p g t", t=4), in_=sample_w.rearrange("(g p t) -> p g t", p=P, t=4)
        )
        nc.scalar.dma_start(out=scale_bc[:], in_=x_scale.rearrange("o k -> (o k)").partition_broadcast(P))
        nc.scalar.activation(dummy[:], dummy[:], ACT.Sin)

        xraw = [kt([P, 4 * K], U8, f"xraw{g}") for g in range(G)]
        oraw = {}
        for q in range(2):
            for h in range(2):
                oraw[(q, h)] = stream.tile([P, 4, 512], BF16, tag="raw", name=f"oraw{q}{h}", bufs=6)
        yraw = {}
        th = [kt([P, ND, T], BF16, f"theta{c}") for c in range(2)]

        def load_x(g, t0=0, t1=4):
            nc.sync.dma_start(
                out=xraw[g][:, K * t0 : K * t1],
                in_=x_bytes[512 * g : 512 * (g + 1), :].rearrange("(p t) k -> p (t k)", t=4)[:, K * t0 : K * t1],
            )

        def load_o(q, h):
            nc.sync.dma_start(
                out=oraw[(q, h)][:],
                in_=omega[512 * q : 512 * (q + 1), 512 * h : 512 * (h + 1)].rearrange("(p j) d -> p j d", j=4),
            )

        load_x(0, 0, 2)
        load_x(0, 2, 4)
        load_o(0, 0)
        load_o(1, 0)
        load_x(1)
        load_o(0, 1)
        load_o(1, 1)
        load_x(2)
        load_x(3)

        def load_y(g):
            yraw[g] = stream.tile([P, 4, T], BF16, tag="raw", name=f"yraw{g}", bufs=6)
            nc.sync.dma_start(out=yraw[g][:], in_=y[512 * g : 512 * (g + 1), :].rearrange("(p j) n -> p j n", j=4))

        def load_theta(c):
            nc.sync.dma_start(out=th[c][:], in_=(theta_cos, theta_sin)[c].rearrange("(d p) n -> p d n", p=P))

        load_y(0)
        load_y(1)

        vec = kt([P, 24], F32, "vec")
        iwt = kt([P, ND], F32, "iwt")
        pht = kt([P, ND], F32, "pht")
        phh = kt([P, ND], F32, "phh")
        rid1 = kt([P, ND], F32, "rid1")
        w1 = kt([P, 16], F32, "w1")
        w2 = kt([P, 16], F32, "w2")

        def make_vectors():
            vt = psum.tile([P, P], BF16, tag="acc", name="vt")
            nc.tensor.transpose(vt[:], vec_rows[:], ident_b[:])
            nc.vector.tensor_copy(out=vec[:], in_=vt[:, 0:24])
            nc.vector.tensor_copy(out=w1[:], in_=w_raw[:])
            nc.vector.tensor_scalar(w2[:], w_raw[:], -2.0, None, ALU.mult)
            nc.vector.tensor_scalar(iwt[:], vec[:, 0:8], 1.0 / TWO_PI, None, ALU.mult)
            nc.vector.tensor_scalar(pht[:], vec[:, 8:16], 1.0 / TWO_PI, None, ALU.mult)
            nc.vector.tensor_scalar(phh[:], vec[:, 8:16], 0.5, None, ALU.mult)
            nc.vector.tensor_scalar(rid1[:], vec[:, 16:24], 1.0, None, ALU.add)

        def interleave(dst, raw, eng):
            dst = dst.rearrange("p (c i j) -> p c j i", i=4, j=4)
            src = raw.rearrange("p j (c i) -> p c j i", i=4)
            if eng == "s":
                nc.scalar.copy(out=dst, in_=src)
            elif eng == "v":
                nc.vector.tensor_copy(out=dst, in_=src)
            else:
                nc.gpsimd.tensor_scalar(dst, src, 1.0, 0.0, ALU.mult, ALU.add)

        qin = {}

        def qin_tile(key):
            qin[key] = stream.tile([P, 2048], BF16, tag="qin", name="qin_" + "_".join(str(e) for e in key), align_bytes=64, bufs=5)
            return qin[key]

        oc = [kt([P, D], U32, f"oc{q}") for q in range(2)]
        osc = [kt([P, D], U8, f"os{q}") for q in range(2)]

        def o_interleave(q, c0, c1, eng):
            if c1 - c0 < 512:
                t = stream.tile([P, 1024], BF16, tag="qsmall", name=f"qsmall{q}{c0}", align_bytes=64, bufs=4)
                qin[("o", q, c0)] = t
            else:
                t = qin_tile(("o", q, c0))
            interleave(t[:, 0 : 4 * (c1 - c0)], oraw[(q, c0 // 512)][:, :, c0 % 512 : c0 % 512 + c1 - c0], eng)

        def o_quant(q, c0, c1):
            nc.vector.quantize_mx(
                out=oc[q][:, c0:c1].bitcast(FP8X4), scales=osc[q][:, c0:c1], in_=qin[("o", q, c0)][:, 0 : 4 * (c1 - c0)]
            )

        yc = [kt([P, T], U32, f"yc{g}") for g in range(G)]
        ys = [kt([P, T], U8, f"ys{g}") for g in range(G)]

        def y_interleave(g, eng):
            t = qin_tile(("y", g))
            interleave(t[:], yraw[g][:], eng)

        def y_quant(g):
            nc.vector.quantize_mx(out=yc[g][:].bitcast(FP8X4), scales=ys[g][:], in_=qin[("y", g)][:])

        xb = {}
        xc = {}
        xs = {}
        for g in range(G):
            for q in range(2):
                xc[(g, q)] = kt([P, 512], U32, f"xc{g}{q}")
                xs[(g, q)] = kt([P, 512], U8, f"xs{g}{q}")

        def x_widen(g, t):
            if t == 0:
                xb[g] = stream.tile([P, 4 * K], BF16, tag="xb", name=f"xb{g}", align_bytes=64, bufs=2)
            c = slice(K * t, K * (t + 1))
            nc.vector.tensor_tensor(xb[g][:, c], xraw[g][:, c].bitcast(FP8), scale_bc[:], ALU.mult)

        def x_transpose(g, q, h, eng="s"):
            if h == 0:
                qin_tile(("x", g, q))
            words = xb[g][:].bitcast(F32)
            bank = psum.tile([P, 2, 2, P], F32, tag="acc", name=f"xt{g}{q}{h}")
            for a in range(2):
                for u in range(2):
                    base = 512 * (2 * h + a) + 256 * q
                    nc.tensor.transpose(bank[:, a, u, :], words[:, base + u : base + 256 : 2], ident_f[:])
            dst = qin[("x", g, q)][:].bitcast(F32)[:, 512 * h : 512 * (h + 1)].rearrange("p (a r u) -> p a r u", a=2, u=2)
            if eng == "s":
                nc.scalar.copy(out=dst, in_=bank[:].rearrange("p a u r -> p a r u"))
            else:
                nc.vector.tensor_copy(out=dst, in_=bank[:].rearrange("p a u r -> p a r u"))

        def x_quant(g, q, lo=0, hi=512):
            nc.vector.quantize_mx(
                out=xc[(g, q)][:, lo:hi].bitcast(FP8X4), scales=xs[(g, q)][:, lo:hi], in_=qin[("x", g, q)][:, 4 * lo : 4 * hi]
            )

        units = [(0, d) for d in range(ND)] + [(1, d) for d in range(ND)]
        for d in range(ND):
            units += [(2, d), (3, d)]
        n_units = len(units)
        last = n_units - 1
        zb, nb, vb, sb, hb, qb, fs, fq, hin = {}, {}, {}, {}, {}, {}, {}, {}, {}
        hcod, hsc = {}, {}
        for u in units:
            hcod[u] = kt([P, 256], U32, f"hc{u[0]}{u[1]}")
            hsc[u] = kt([P, 256], U8, f"hs{u[0]}{u[1]}")
        stats = [kt([P, 2 * G], F32, f"stats{d}") for d in range(ND)]

        def z_mm(i, lo=0, hi=512):
            g, d = units[i]
            if lo == 0:
                zb[i] = psum.tile([P, 512], F32, tag="z", name=f"z{i}", bufs=3)
            c = slice(P * d, P * (d + 1))
            for q in range(2):
                nc.tensor.matmul_mx(
                    out=zb[i][:, lo:hi], lhsT=oc[q][:, c].bitcast(FP8X4), lhsT_scale=osc[q][:, c],
                    rhs=xc[(g, q)][:, lo:hi].bitcast(FP8X4), rhs_scale=xs[(g, q)][:, lo:hi], start=(q == 0), stop=(q == 1),
                )

        def rr1(i, lo=0, hi=512):
            d = units[i][1]
            if lo == 0:
                nb[i] = stream.tile([P, 512], I32, tag="n", name=f"n{i}")
            if i in via_g or i in via_v:
                u = stream.tile([P, 512], F32, tag="u", name=f"u{i}", bufs=2)
                nc.scalar.activation(u[:, lo:hi], zb[i][:, lo:hi], ACT.Identity, bias=pht[:, d : d + 1], scale=iwt[:, d : d + 1])
                if i in via_g:
                    nc.gpsimd.tensor_scalar(nb[i][:, lo:hi], u[:, lo:hi], 1.0, 0.0, ALU.mult, ALU.add)
                else:
                    nc.vector.tensor_copy(out=nb[i][:, lo:hi], in_=u[:, lo:hi])
            else:
                nc.vector.tensor_scalar(
                    nb[i][:, lo:hi], zb[i][:, lo:hi], iwt[:, d : d + 1], pht[:, d : d + 1], ALU.mult, ALU.add
                )

        def rr2(i, lo=0, hi=512):
            d = units[i][1]
            if lo == 0:
                vb[i] = stream.tile([P, 512], F32, tag="v", name=f"v{i}", bufs=3)
            nc.vector.scalar_tensor_tensor(
                vb[i][:, lo:hi], zb[i][:, lo:hi], iwt[:, d : d + 1], nb[i][:, lo:hi], ALU.mult, ALU.subtract
            )

        def sines(i, lo=0, hi=512):
            d = units[i][1]
            if lo == 0:
                hb[i] = stream.tile([P, 512], F32, tag="half", name=f"half{i}", bufs=2)
                sb[i] = stream.tile([P, 512], F32, tag="sin", name=f"sin{i}", bufs=2)
            nc.scalar.activation(hb[i][:, lo:hi], vb[i][:, lo:hi], ACT.Sin, bias=phh[:, d : d + 1], scale=math.pi)
            nc.scalar.activation(sb[i][:, lo:hi], vb[i][:, lo:hi], ACT.Sin, bias=vec[:, 8 + d : 9 + d], scale=TWO_PI)

        def square_half(i, eng="s"):
            qb[i] = stream.tile([P, 512], F32, tag="q", name=f"q{i}", bufs=2)
            if eng == "v":
                nc.vector.tensor_tensor(qb[i][:], hb[i][:], hb[i][:], ALU.mult)
            elif eng == "g":
                nc.gpsimd.tensor_tensor(qb[i][:], hb[i][:], hb[i][:], ALU.mult)
            else:
                nc.scalar.activation(qb[i][:], hb[i][:], ACT.Square)

        def square_sum(i):
            g, d = units[i]
            junk = stream.tile([P, 512], BF16, tag="junk", name=f"junk{i}", bufs=2)
            nc.scalar.activation(junk[:], sb[i][:], ACT.Square, accum_out=stats[d][:, g : g + 1])

        def trans_s(i):
            fs[i] = psum.tile([P, 4, P], F32, tag="f", name=f"fs{i}", bufs=3)
            for t in range(4):
                nc.tensor.transpose(fs[i][:, t, :], sb[i][:, P * t : P * (t + 1)], ident_f[:])

        def trans_q(i):
            fq[i] = psum.tile([P, 4, P], F32, tag="f", name=f"fq{i}", bufs=3)
            for t in range(4):
                nc.tensor.transpose(fq[i][:, t, :], qb[i][:, P * t : P * (t + 1)], ident_f[:])

        def hin_tile(i):
            if i not in hin:
                hin[i] = stream.tile([P, 1024], BF16, tag="hin", name=f"hin{i}", align_bytes=64, bufs=3)
            return hin[i]

        def w_s(i):
            g = units[i][0]
            nc.vector.tensor_tensor(
                hin_tile(i)[:, 512:1024].rearrange("p (d t) -> p d t", t=4),
                fs[i][:].rearrange("p t d -> p d t"),
                w1[:, 4 * g : 4 * g + 4].unsqueeze(1).to_broadcast([P, P, 4]),
                ALU.mult,
            )

        def w_c(i):
            g = units[i][0]
            nc.vector.scalar_tensor_tensor(
                hin_tile(i)[:, 0:512].rearrange("p (d t) -> p d t", t=4),
                fq[i][:].rearrange("p t d -> p d t"),
                0.5,
                w2[:, 4 * g : 4 * g + 4].unsqueeze(1).to_broadcast([P, P, 4]),
                ALU.subtract,
                ALU.mult,
            )

        def f_quant(i, lo=0, hi=256):
            u = units[i]
            nc.vector.quantize_mx(
                out=hcod[u][:, lo:hi].bitcast(FP8X4), scales=hsc[u][:, lo:hi], in_=hin[i][:, 4 * lo : 4 * hi]
            )

        acc, rec, dens = {}, {}, {}

        def moments(d, groups=range(G), which=(0, 1)):
            for c in which:
                if groups[0] == 0:
                    acc[(c, d)] = psum.tile([P, T], F32, tag="acc", name=f"acc{c}{d}")
                cols = slice(P * c, P * (c + 1))
                for g in groups:
                    nc.tensor.matmul_mx(
                        out=acc[(c, d)][:], lhsT=hcod[(g, d)][:, cols].bitcast(FP8X4), lhsT_scale=hsc[(g, d)][:, cols],
                        rhs=yc[g][:].bitcast(FP8X4), rhs_scale=ys[g][:], start=(g == 0), stop=(g == G - 1),
                    )

        def denominators(d):
            es = stream.tile([P, 4], F32, tag="es", name=f"es{d}")
            dens[d] = stream.tile([P, 2], F32, tag="den", name=f"den{d}")
            nc.gpsimd.tensor_tensor(es[:, 0:2], stats[d][:, 0:2], stats[d][:, 2:4], ALU.add)
            nc.gpsimd.tensor_tensor(es[:, 2:3], es[:, 0:1], es[:, 1:2], ALU.add)
            nc.gpsimd.tensor_scalar(dens[d][:, 0:1], es[:, 2:3], -1.0 / M, rid1[:, d : d + 1], ALU.mult, ALU.add)
            nc.gpsimd.tensor_scalar(dens[d][:, 1:2], es[:, 2:3], 1.0 / M, vec[:, 16 + d : 17 + d], ALU.mult, ALU.add)

        def recip(d):
            rec[d] = stream.tile([P, 2], F32, tag="rec", name=f"rec{d}", bufs=3)
            nc.vector.reciprocal(rec[d][:], dens[d][:])

        def epilogue(d, which=(0, 1), parts=1):
            for c in which:
                o = stream.tile([P, T], F32, tag="o", name=f"o{c}{d}", bufs=4)
                w = T // parts
                for k in range(parts):
                    cs = slice(w * k, w * (k + 1))
                    nc.vector.scalar_tensor_tensor(
                        o[:, cs], acc[(c, d)][:, cs], rec[d][:, c : c + 1], th[c][:, d, cs], ALU.mult, ALU.add
                    )
                    nc.sync.dma_start(out=(out_0, out_1)[c][P * d : P * (d + 1), cs], in_=o[:, cs])

        via_g = PRM.get("via_g", ())
        via_v = PRM.get("via_v", ())
        extra = {}

        def at(step, fn, *args):
            extra.setdefault(step, []).append((fn, args))

        make_vectors()
        x_widen(0, 0)
        x_widen(0, 1)
        o_interleave(0, 0, 128, PRM["oe"][0])
        o_interleave(1, 0, 128, PRM["oe"][1])
        x_transpose(0, 0, 0)
        x_transpose(0, 1, 0)
        x_widen(0, 2)
        x_widen(0, 3)
        x_quant(0, 0, 0, 256)
        x_quant(0, 1, 0, 256)
        o_quant(0, 0, 128)
        o_quant(1, 0, 128)
        x_transpose(0, 0, 1)
        x_transpose(0, 1, 1)
        z_mm(0, 0, 256)
        x_widen(1, 0)
        rr1(0, 0, 256)
        x_quant(0, 0, 256, 512)
        rr2(0, 0, 256)
        x_quant(0, 1, 256, 512)
        z_mm(0, 256, 512)
        o_interleave(0, 128, 256, PRM["oe"][2])
        o_interleave(1, 128, 256, PRM["oe"][3])
        sines(0, 0, 256)
        x_widen(1, 1)
        rr1(0, 256, 512)
        o_quant(0, 128, 256)
        o_quant(1, 128, 256)
        z_mm(1)
        rr2(0, 256, 512)
        sines(0, 256, 512)
        o_interleave(0, 256, 512, PRM["oe"][4])
        o_interleave(1, 256, 512, PRM["oe"][5])
        rr1(1)
        x_widen(1, 2)
        o_quant(0, 256, 512)
        o_quant(1, 256, 512)
        a = PRM["o1"]
        at(a, o_interleave, 0, 512, 1024, PRM["oe"][6])
        at(a, o_interleave, 1, 512, 1024, PRM["oe"][7])
        at(a + 1, o_quant, 0, 512, 1024)
        at(a + 1, o_quant, 1, 512, 1024)
        for g in (2, 3):
            at(2, load_y, g)
        for c in range(2):
            at(2, load_theta, c)
        for g in (1, 2, 3):
            ws, ts, qs = PRM["x"][g - 1]
            for t in range(3 if g == 1 else 0, 4):
                at(ws[t], x_widen, g, t)
            for k, (q, h) in enumerate(((0, 0), (1, 0), (0, 1), (1, 1))):
                at(ts[k], x_transpose, g, q, h)
            at(qs[0], x_quant, g, 0)
            at(qs[1], x_quant, g, 1)
        for g in range(G):
            at(PRM["y"][g], y_interleave, g, PRM["ye"][g])
            at(PRM["y"][g] + PRM.get("yl", 2), y_quant, g)

        for i in range(n_units + 3):
            if i + 2 < n_units:
                z_mm(i + 2)
            if 0 < i and i + 1 < n_units:
                rr1(i + 1)
            if 0 <= i - 4 and units[i - 4][0] == 3:
                moments(units[i - 4][1], [3])
            if 0 <= i - 2:
                w_s(i - 2)
            if i < n_units:
                if i > 0:
                    rr2(i)
                    sines(i)
                square_half(i, PRM["qe"].get(i, "s") if i < last else "v")
                square_sum(i)
                if units[i][0] == 3:
                    denominators(units[i][1])
            if 0 <= i - 1 < n_units:
                if i - 1 == last:
                    trans_q(i - 1)
                    trans_s(i - 1)
                else:
                    trans_s(i - 1)
                    trans_q(i - 1)
            if 0 <= i - 3 and units[i - 3][0] == 3:
                moments(units[i - 3][1], [0, 1, 2])
            if 0 <= i - 2 < last:
                w_c(i - 2)
            for fn, args in extra.get(i, []):
                fn(*args)
            if 0 <= i - 3:
                f_quant(i - 3)
                if units[i - 3][0] == 3:
                    recip(units[i - 3][1])
            if 0 <= i - 4 and units[i - 4][0] == 3:
                epilogue(units[i - 4][1])
            if i == n_units:
                moments(ND - 2, [3])
                w_c(last)
                f_quant(last - 1)
                epilogue(ND - 2)
                f_quant(last, 0, 128)
                moments(ND - 1, [0, 1, 2])
                w_s(last)
                recip(ND - 1)
                moments(ND - 1, [3], [0])
                f_quant(last, 128, 256)
                moments(ND - 1, [3], [1])
                epilogue(ND - 1, [0], 2)
                epilogue(ND - 1, [1], 2)
                break
